import numpy as np
import ml_dtypes


def mxq(x, axis, fmt="e4m3"):
    dtype, down = {"e4m3": (ml_dtypes.float8_e4m3fn, 7), "e5m2": (ml_dtypes.float8_e5m2, 14)}[fmt]
    v = np.moveaxis(np.asarray(x, np.float32).astype(ml_dtypes.bfloat16).astype(np.float64), axis, -1)
    blocks = v.reshape(v.shape[:-1] + (-1, 32))
    amax = np.abs(blocks).max(-1, keepdims=True)
    byte = np.maximum(np.where(amax > 0, np.frexp(amax)[1] - 1 + 127, 0) - down, 1)
    scale = np.exp2(byte - 127.0)
    codes = (blocks / scale).astype(np.float32).astype(dtype).astype(np.float64)
    return np.moveaxis((codes * scale).reshape(v.shape), -1, axis)


WIDE = False


def mx_kscale(k):
    if not WIDE:
        return np.ones(k)
    levels = np.array([10, -10, 5, -5, 0])
    if k % 512:
        return np.exp2(np.random.permutation(np.resize(levels, k // 32))).repeat(32)
    a = np.empty((k // 512, 16))
    for p in range(k // 512):
        a[p, :8] = np.random.permutation(np.resize(levels, 8))
        for g in range(8):
            far = levels[np.abs(levels - a[p, g]) >= 10]
            a[p, g + 8] = far[np.random.randint(len(far))]
    return np.exp2(a.ravel()).repeat(32)


def f64(x):
    return np.asarray(x).astype(np.float64)


def striped(idx):
    return np.tile(idx.reshape(-1, 16).T, (8, 1)).astype(np.uint16)


def unstriped(offs):
    return offs[:16].T.reshape(-1).astype(np.int64)


E2M1 = np.array([0.0, 0.5, 1.0, 1.5, 2.0, 3.0, 4.0, 6.0, -0.0, -0.5, -1.0, -1.5, -2.0, -3.0, -4.0, -6.0])


def pack_weight(w, fmt):
    k, n = w.shape
    w = f64(np.asarray(w, np.float32).astype(ml_dtypes.bfloat16)).reshape(k // 32, 32, n)
    amax = np.abs(w).max(1)
    if fmt == "e4m3":
        byte = np.frexp(amax)[1] - 1 + 127 - 7
    else:
        mant, ex = np.frexp(amax / 6.0)
        byte = np.where(mant > 0.5, ex, ex - 1) + 127
    byte = np.clip(np.where(amax > 0, byte, 1), 1, 254)
    scaled = (w * np.exp2(127.0 - byte)[:, None, :]).reshape(k, n).astype(np.float32)
    by_word = np.ascontiguousarray(scaled.reshape(k // 512, 128, 4, n).transpose(0, 1, 3, 2))
    if fmt == "e4m3":
        words = by_word.astype(ml_dtypes.float8_e4m3fn).view(np.uint8)
    else:
        c = by_word.astype(ml_dtypes.float4_e2m1fn).view(np.uint8) & 0xF
        words = (c[..., 0::2] | (c[..., 1::2] << 4)).reshape(k // 512, 128, 2 * n)
    return np.ascontiguousarray(words), np.ascontiguousarray(byte.astype(np.uint8).reshape(k // 512, 16, n))


def unpack_weight(words, scales, fmt):
    g, _, n = scales.shape
    words = np.ascontiguousarray(words).reshape(g, 128, n, -1)
    if fmt == "e4m3":
        vals = words.view(ml_dtypes.float8_e4m3fn).astype(np.float64)
    else:
        nib = np.empty((g, 128, n, 4), np.uint8)
        nib[..., 0::2] = words & 0xF
        nib[..., 1::2] = words >> 4
        vals = E2M1[nib]
    vals = vals * np.repeat(np.exp2(scales.astype(np.float64) - 127.0), 8, axis=1)[..., None]
    return vals.transpose(0, 1, 3, 2).reshape(g * 512, n)


def relu2(v):
    return np.maximum(v, 0.0) ** 2


K, T, E, C, N = 512, 512, 8, 128, 256
M = 1024


def by_expert(wq, xq):
    return np.concatenate([wq[e].T @ xq[:, e * C:(e + 1) * C] for e in range(E)], axis=1)


def setup_inputs():
    n = np.random.standard_normal
    s = mx_kscale(K)[:, None]
    first = np.random.permutation(np.repeat(np.arange(E), T // E))
    second = (first + 1 + np.random.permutation(np.repeat(np.arange(E - 1), -(-T // (E - 1)))[:T])) % E
    while np.bincount(second, minlength=E).max() != T // E:
        load = np.bincount(second, minlength=E); hi, lo = int(load.argmax()), int(load.argmin())
        t = np.flatnonzero((second == hi) & (first != lo))[0]; second[t] = lo
    slot_token = np.empty(E * C, np.int64); pos = np.empty((2, T), np.int64); fill = np.zeros(E, np.int64)
    place = np.stack([np.random.permutation(C) for _ in range(E)])
    for r, deal in enumerate((first, second)):
        for t in np.random.permutation(T):
            e = deal[t]; j = e * C + place[e, fill[e]]; fill[e] += 1; slot_token[j] = t; pos[r, t] = j
    g = np.random.uniform(0.2, 0.8, T)
    w = [pack_weight(m, "e2m1") for m in n((E, K, N)) / np.sqrt(K) / s[None]]
    r = mx_kscale(M)[:, None]
    return {
        "uT": (n((M, T)) * r).astype(np.float32),
        "wu": (n((M, K)) / np.sqrt(M) / r * s.T).astype(np.float32),
        "w_words": np.stack([m[0] for m in w]),
        "w_scales": np.stack([m[1] for m in w]),
        "b": (0.3 * n((N, E))).astype(np.float32),
        "gate": np.stack([np.tile(g, (N, 1)), np.tile(1.0 - g, (N, 1))]).astype(np.float32),
        "offs": striped(slot_token),
        "pos1": striped(pos[0]),
        "pos2": striped(pos[1]),
    }


def reference(uT, wu, w_words, w_scales, b, gate, offs, pos1, pos2):
    idx = unstriped(offs)
    w = np.stack([unpack_weight(w_words[e], w_scales[e], "e2m1") for e in range(E)])
    x = mxq(f64(wu), 0, "e4m3").T @ mxq(f64(uT), 0, "e4m3")
    xq = mxq(x[:, idx], 0, "e4m3")
    y = by_expert(w, xq)
    y = relu2(y + np.repeat(f64(b), C, axis=1))
    return f64(gate[0]) * y[:, unstriped(pos1)] + f64(gate[1]) * y[:, unstriped(pos2)]

@@ -1,0 +1,209 @@
+from contextlib import ExitStack
+
+import concourse.mybir as mybir
+
+F, K, T, E, C, N = 1024, 512, 512, 8, 128, 256
+S = E * C
+
+FLOPS = 2 * F * K * T + 2 * K * N * S
+
+F32 = mybir.dt.float32
+BF16 = mybir.dt.bfloat16
+I32 = mybir.dt.int32
+U32 = mybir.dt.uint32
+U16 = mybir.dt.uint16
+U8 = mybir.dt.uint8
+FP8X4 = mybir.dt.float8_e4m3fn_x4
+FP4X4 = mybir.dt.float4_e2m1fn_x4
+ACT = mybir.ActivationFunctionType
+ALU = mybir.AluOpType
+
+P = 128
+PACK = 4
+PASS = P * PACK
+HALF = T // 2
+U_VECTOR = 128
+W_VECTOR = 64
+CHUNKS = (256, 256, 256, 128, 128)
+
+
+def tile_moe_prv_lin_relu2_kernel(
+    tc, uT, wu, w_words, w_scales, b, gate, offs, pos1, pos2, out
+):
+    nc = tc.nc
+    with ExitStack() as ctx:
+        keep = ctx.enter_context(tc.tile_pool(name="keep", bufs=1))
+        psum = ctx.enter_context(tc.psum_pool(name="psum", bufs=1))
+
+        wu_raw = []
+        for a in range(2):
+            raw = keep.tile([P, PACK, K], F32, name=f"wu_raw{a}")
+            nc.sync.dma_start(out=raw[:], in_=wu[a * PASS:(a + 1) * PASS, :].rearrange("(p j) c -> p j c", j=PACK))
+            wu_raw.append(raw)
+        u_raw = {}
+        for h in range(2):
+            for a in range(2):
+                raw = keep.tile([P, PACK, HALF], F32, name=f"u_raw{h}{a}")
+                nc.sync.dma_start(
+                    out=raw[:],
+                    in_=uT[a * PASS:(a + 1) * PASS, h * HALF:(h + 1) * HALF].rearrange("(p j) c -> p j c", j=PACK),
+                )
+                u_raw[h, a] = raw
+        offs_sb = keep.tile([P, S // 16], U16, name="offs_sb")
+        nc.sync.dma_start(offs_sb[:], offs)
+        ww = keep.tile([P, E * 2 * N], U8, name="ww", align_bytes=64)
+        nc.sync.dma_start(
+            out=ww[:].bitcast(I32).rearrange("p (e n) -> p e n", e=E),
+            in_=w_words.bitcast(I32).rearrange("e a p n -> p (e a) n"),
+        )
+        ws = keep.tile([P, E * N], U8, name="ws", align_bytes=64)
+        nc.gpsimd.memset(ws[:].bitcast(I32), 0)
+        rows = w_scales.bitcast(I32).rearrange("e a (q r) n -> r q (e a) n", r=4)
+        for r in range(4):
+            nc.sync.dma_start(out=ws[r:P:32, :].bitcast(I32).rearrange("q (e n) -> q e n", e=E), in_=rows[r])
+        bias = keep.tile([P, 2, E], F32, name="bias")
+        nc.sync.dma_start(out=bias[:], in_=b.rearrange("(h p) e -> p h e", p=P))
+        gate_sb = keep.tile([P, 2, T], F32, name="gate_sb")
+        nc.sync.dma_start(out=gate_sb[:], in_=gate[:, 0:P, :].rearrange("r p t -> p r t"))
+        pos_sb = []
+        for r, pos in enumerate((pos1, pos2)):
+            lst = keep.tile([P, T // 16], U16, name=f"pos_sb{r}")
+            nc.sync.dma_start(lst[:], pos)
+            pos_sb.append(lst)
+
+        def quantise(grouped, width, name):
+            codes = keep.tile([P, width], U32, name=f"{name}_codes", align_bytes=64)
+            scales = keep.tile([P, width], U8, name=f"{name}_scales", align_bytes=64)
+            nc.vector.quantize_mx(out=codes[:].bitcast(FP8X4), scales=scales[:], in_=grouped)
+            return codes, scales
+
+        wu_q = []
+        for a in range(2):
+            grouped = keep.tile([P, K * PACK], BF16, name=f"wu_grouped{a}", align_bytes=64)
+            dst = grouped[:].rearrange("p (t m j) -> p m j t", t=PACK, j=PACK)
+            src = wu_raw[a][:].rearrange("p j (m t) -> p m j t", t=PACK)
+            nc.vector.tensor_copy(out=dst[:, :W_VECTOR], in_=src[:, :W_VECTOR])
+            nc.scalar.copy(out=dst[:, W_VECTOR:], in_=src[:, W_VECTOR:])
+            wu_q.append(quantise(grouped[:], K, f"wu{a}"))
+
+        pairs = [keep.tile([P, T * 2], BF16, name=f"pairs{g}", align_bytes=64) for g in range(2)]
+        for h in range(2):
+            u_q = []
+            for a in range(2):
+                grouped = keep.tile([P, HALF * PACK], BF16, name=f"u_grouped{h}{a}", align_bytes=64)
+                dst = grouped[:].rearrange("p (c i j) -> p c j i", i=4, j=PACK)
+                src = u_raw[h, a][:].rearrange("p j (c i) -> p c j i", i=4)
+                if (h, a) == (1, 1):
+                    nc.vector.tensor_copy(out=dst, in_=src)
+                else:
+                    cut = U_VECTOR // 4
+                    nc.vector.tensor_copy(out=dst[:, :cut], in_=src[:, :cut])
+                    nc.scalar.copy(out=dst[:, cut:], in_=src[:, cut:])
+                u_q.append(quantise(grouped[:], HALF, f"u{h}{a}"))
+            banks = [psum.tile([P, 2, HALF], F32, name=f"x_bank{h}{g}") for g in range(2)]
+
+            def project(g, j, a):
+                cols = slice((2 * g + j) * P, (2 * g + j + 1) * P)
+                nc.tensor.matmul_mx(
+                    out=banks[g][:, j, :],
+                    lhsT=wu_q[a][0][:, cols].bitcast(FP8X4),
+                    lhsT_scale=wu_q[a][1][:, cols],
+                    rhs=u_q[a][0][:].bitcast(FP8X4),
+                    rhs_scale=u_q[a][1][:],
+                    start=(a == 0),
+                    stop=(a == 1),
+                )
+
+            for g in range(2):
+                project(g, 0, 0)
+            for g in range(2):
+                project(g, 0, 1)
+                project(g, 1, 0)
+                project(g, 1, 1)
+                dst = pairs[g][:, h * T:(h + 1) * T].rearrange("p (n j) -> p n j", j=2)
+                src = banks[g][:].rearrange("p j n -> p n j")
+                if g == 0 and h == 1:
+                    nc.vector.tensor_copy(out=dst, in_=src)
+                else:
+                    nc.scalar.copy(out=dst, in_=src)
+
+        relu = [keep.tile([P, S], F32, name=f"relu{nb}") for nb in range(2)]
+        y = [keep.tile([P, S], F32, name=f"y{nb}") for nb in range(2)]
+        slot_q = []
+
+        def expert(bank_cols, e, nb):
+            codes, scales, first = slot_q[e]
+            w0 = e * N + nb * P
+            nc.tensor.matmul_mx(
+                out=bank_cols,
+                lhsT=ww[:, 2 * w0:2 * (w0 + P)].bitcast(FP4X4),
+                lhsT_scale=ws[:, w0:w0 + P],
+                rhs=codes[:, first:first + C].bitcast(FP8X4),
+                rhs_scale=scales[:, first:first + C],
+                start=True,
+                stop=True,
+            )
+
+        def rectify(bank_cols, e, nb):
+            nc.scalar.activation(
+                out=relu[nb][:, e * C:(e + 1) * C], in_=bank_cols, func=ACT.Relu, bias=bias[:, nb, e:e + 1]
+            )
+
+        def square(nb, s0, s1):
+            nc.scalar.activation(out=y[nb][:, s0:s1], in_=relu[nb][:, s0:s1], func=ACT.Square)
+
+        starts = [sum(CHUNKS[:c]) for c in range(len(CHUNKS))]
+        last = len(CHUNKS) - 1
+        woven = {}
+
+        def gather(c):
+            width = CHUNKS[c]
+            entries = offs_sb[:, starts[c] // 16:(starts[c] + width) // 16]
+            woven[c] = keep.tile([P, width * 2], U32, name=f"woven{c}", tag=f"stage{c - 2 if c == last else c}", align_bytes=64)
+            side_by_side = woven[c][:].rearrange("p (n g) -> p n g", g=2)
+            if c == last:
+                for g in range(2):
+                    nc.vector.tensor_copy(out=side_by_side[:, :, g], in_=pairs[g][:].bitcast(U32).indirect(entries))
+                return
+            picked = keep.tile([P, 2, width], U32, name=f"picked{c}", tag=f"stage{c - 2}", align_bytes=64)
+            for g in range(2):
+                nc.vector.tensor_copy(out=picked[:, g, :], in_=pairs[g][:].bitcast(U32).indirect(entries))
+            nc.scalar.copy(out=side_by_side, in_=picked[:].rearrange("p g n -> p n g"))
+
+        def multiply(c):
+            width = CHUNKS[c]
+            codes, scales = quantise(woven[c][:].bitcast(BF16), width, f"x{c}")
+            bank = psum.tile([P, width], F32, name=f"y0_bank{c}", tag="x_bank00" if c == last else f"y0_bank{c}")
+            for i in range(width // C):
+                slot_q.append((codes, scales, i * C))
+                expert(bank[:, i * C:(i + 1) * C], starts[c] // C + i, 0)
+            return bank
+
+        def finish(c, bank):
+            for i in range(CHUNKS[c] // C):
+                rectify(bank[:, i * C:(i + 1) * C], starts[c] // C + i, 0)
+            square(0, starts[c], starts[c] + CHUNKS[c])
+
+        gather(0)
+        gather(1)
+        for c in range(len(CHUNKS)):
+            bank = multiply(c)
+            if c + 2 <= last:
+                gather(c + 2)
+            finish(c, bank)
+
+        for q in (1, 0):
+            bank = psum.tile([P, 4 * C], F32, name=f"y1_bank{q}", tag="x_bank01" if q == 1 else f"y0_bank{last - 1}")
+            for i in range(4):
+                expert(bank[:, i * C:(i + 1) * C], 4 * q + i, 1)
+            for i in range(4):
+                rectify(bank[:, i * C:(i + 1) * C], 4 * q + i, 1)
+            square(1, q * 4 * C, (q + 1) * 4 * C)
+
+        for nb in range(2):
+            terms = keep.tile([P, 2, T], F32, name=f"terms{nb}")
+            for r in range(2):
+                nc.vector.tensor_tensor(terms[:, r, :], y[nb][:].indirect(pos_sb[r][:]), gate_sb[:, r, :], ALU.mult)
+            total = keep.tile([P, T], F32, name=f"total{nb}")
+            nc.vector.tensor_tensor(total[:], terms[:, 0, :], terms[:, 1, :], ALU.add)
+            nc.sync.dma_start(out=out[nb * P:(nb + 1) * P, :], in_=total[:])

@@ -1,6 +1,7 @@
 from contextlib import ExitStack
 
 import concourse.mybir as mybir
+from concourse.masks import make_identity
 
 F, K, T, E, C, N = 1024, 512, 512, 8, 128, 256
 S = E * C
@@ -25,6 +26,10 @@ HALF = T // 2
 U_VECTOR = 128
 W_VECTOR = 64
 CHUNKS = (256, 256, 256, 128, 128)
+WOVEN_TAGS = ("chain0", "chain1", "chain2", "chain3", "chain2")
+PICKED_TAGS = ("picked0", "picked1", "chain0", "chain1")
+RELU_TAGS = ("relu00", "relu01", "relu02")
+Y0_BANKS = ("spare0", "spare1", "x_bank0_0", "x_bank1_0", "x_bank0_256")
 
 
 def tile_moe_prv_lin_relu2_kernel(
@@ -63,16 +68,22 @@ def tile_moe_prv_lin_relu2_kernel(
             nc.sync.dma_start(out=ws[r:P:32, :].bitcast(I32).rearrange("q (e n) -> q e n", e=E), in_=rows[r])
         bias = keep.tile([P, 2, E], F32, name="bias")
         nc.sync.dma_start(out=bias[:], in_=b.rearrange("(h p) e -> p h e", p=P))
-        gate_sb = keep.tile([P, 2, T], F32, name="gate_sb")
-        nc.sync.dma_start(out=gate_sb[:], in_=gate[:, 0:P, :].rearrange("r p t -> p r t"))
+        gate_cols = keep.tile([P, 2, 8], F32, name="gate_cols")
+        with nc.allow_non_contiguous_dma(reason="one gate value a token, a token a partition"):
+            for r in range(2):
+                nc.sync.dma_start(out=gate_cols[:, r, 0:4], in_=gate[r, N - 1, :].rearrange("(i p) -> p i", p=P))
+        gate_rows = keep.tile([P, 2, T], F32, name="gate_rows")
+        nc.sync.dma_start(out=gate_rows[:], in_=gate[:, 0:P, :].rearrange("r p t -> p r t"))
+        ident = keep.tile([P, P], F32, name="ident")
+        make_identity(nc, ident[:])
         pos_sb = []
         for r, pos in enumerate((pos1, pos2)):
             lst = keep.tile([P, T // 16], U16, name=f"pos_sb{r}")
             nc.sync.dma_start(lst[:], pos)
             pos_sb.append(lst)
 
-        def quantise(grouped, width, name):
-            codes = keep.tile([P, width], U32, name=f"{name}_codes", align_bytes=64)
+        def quantise(grouped, width, name, tag=None):
+            codes = keep.tile([P, width], U32, name=f"{name}_codes", tag=tag or f"{name}_codes", align_bytes=64)
             scales = keep.tile([P, width], U8, name=f"{name}_scales", align_bytes=64)
             nc.vector.quantize_mx(out=codes[:].bitcast(FP8X4), scales=scales[:], in_=grouped)
             return codes, scales
@@ -87,47 +98,62 @@ def tile_moe_prv_lin_relu2_kernel(
             wu_q.append(quantise(grouped[:], K, f"wu{a}"))
 
         pairs = [keep.tile([P, T * 2], BF16, name=f"pairs{g}", align_bytes=64) for g in range(2)]
-        for h in range(2):
-            u_q = []
-            for a in range(2):
-                grouped = keep.tile([P, HALF * PACK], BF16, name=f"u_grouped{h}{a}", align_bytes=64)
-                dst = grouped[:].rearrange("p (c i j) -> p c j i", i=4, j=PACK)
-                src = u_raw[h, a][:].rearrange("p j (c i) -> p c j i", i=4)
-                if (h, a) == (1, 1):
-                    nc.vector.tensor_copy(out=dst, in_=src)
-                else:
-                    cut = U_VECTOR // 4
-                    nc.vector.tensor_copy(out=dst[:, :cut], in_=src[:, :cut])
-                    nc.scalar.copy(out=dst[:, cut:], in_=src[:, cut:])
-                u_q.append(quantise(grouped[:], HALF, f"u{h}{a}"))
-            banks = [psum.tile([P, 2, HALF], F32, name=f"x_bank{h}{g}") for g in range(2)]
 
-            def project(g, j, a):
-                cols = slice((2 * g + j) * P, (2 * g + j + 1) * P)
-                nc.tensor.matmul_mx(
-                    out=banks[g][:, j, :],
-                    lhsT=wu_q[a][0][:, cols].bitcast(FP8X4),
-                    lhsT_scale=wu_q[a][1][:, cols],
-                    rhs=u_q[a][0][:].bitcast(FP8X4),
-                    rhs_scale=u_q[a][1][:],
-                    start=(a == 0),
-                    stop=(a == 1),
-                )
+        def interleave(h, a, name, t0, t1, split):
+            grouped = keep.tile([P, (t1 - t0) * PACK], BF16, name=f"{name}_grouped", align_bytes=64)
+            dst = grouped[:].rearrange("p (c i j) -> p c j i", i=4, j=PACK)
+            src = u_raw[h, a][:, :, t0:t1].rearrange("p j (c i) -> p c j i", i=4)
+            if split:
+                cut = U_VECTOR // 4
+                nc.vector.tensor_copy(out=dst[:, :cut], in_=src[:, :cut])
+                nc.scalar.copy(out=dst[:, cut:], in_=src[:, cut:])
+            else:
+                nc.vector.tensor_copy(out=dst, in_=src)
+            return grouped
 
+        def project(bank, g, j, a, operand):
+            codes, scales = operand
+            cols = slice((2 * g + j) * P, (2 * g + j + 1) * P)
+            nc.tensor.matmul_mx(
+                out=bank[:, j, :],
+                lhsT=wu_q[a][0][:, cols].bitcast(FP8X4),
+                lhsT_scale=wu_q[a][1][:, cols],
+                rhs=codes.bitcast(FP8X4),
+                rhs_scale=scales,
+                start=(a == 0),
+                stop=(a == 1),
+            )
+
+        def project_tokens(groups):
+            banks = {}
             for g in range(2):
-                project(g, 0, 0)
+                for t0, width, operands in groups:
+                    banks[g, t0] = psum.tile([P, 2, width], F32, name=f"x_bank{g}_{t0}")
+                    project(banks[g, t0], g, 0, 0, operands[0])
             for g in range(2):
-                project(g, 0, 1)
-                project(g, 1, 0)
-                project(g, 1, 1)
-                dst = pairs[g][:, h * T:(h + 1) * T].rearrange("p (n j) -> p n j", j=2)
-                src = banks[g][:].rearrange("p j n -> p n j")
-                if g == 0 and h == 1:
-                    nc.vector.tensor_copy(out=dst, in_=src)
-                else:
-                    nc.scalar.copy(out=dst, in_=src)
+                for t0, width, operands in groups:
+                    for j, a in ((0, 1), (1, 0), (1, 1)):
+                        project(banks[g, t0], g, j, a, operands[a])
+                    nc.scalar.copy(
+                        out=pairs[g][:, 2 * t0:2 * (t0 + width)].rearrange("p (n j) -> p n j", j=2),
+                        in_=banks[g, t0][:].rearrange("p j n -> p n j"),
+                    )
 
-        relu = [keep.tile([P, S], F32, name=f"relu{nb}") for nb in range(2)]
+        first = []
+        for a in range(2):
+            codes, scales = quantise(interleave(0, a, f"u0{a}", 0, HALF, True)[:], HALF, f"u0{a}")
+            first.append((codes[:], scales[:]))
+        project_tokens([(0, HALF, first)])
+        codes0, scales0 = quantise(interleave(1, 0, "u10", 0, HALF, True)[:], HALF, "u10")
+        staged = [interleave(1, 1, f"u11{i}", i * P, (i + 1) * P, False) for i in range(2)]
+        groups = []
+        for i in range(2):
+            codes, scales = quantise(staged[i][:], P, f"u11{i}")
+            cols = slice(i * P, (i + 1) * P)
+            groups.append((HALF + i * P, P, [(codes0[:, cols], scales0[:, cols]), (codes[:], scales[:])]))
+        project_tokens(groups)
+
+
         y = [keep.tile([P, S], F32, name=f"y{nb}") for nb in range(2)]
         slot_q = []
 
@@ -144,66 +170,107 @@ def tile_moe_prv_lin_relu2_kernel(
                 stop=True,
             )
 
-        def rectify(bank_cols, e, nb):
-            nc.scalar.activation(
-                out=relu[nb][:, e * C:(e + 1) * C], in_=bank_cols, func=ACT.Relu, bias=bias[:, nb, e:e + 1]
-            )
-
-        def square(nb, s0, s1):
-            nc.scalar.activation(out=y[nb][:, s0:s1], in_=relu[nb][:, s0:s1], func=ACT.Square)
+        def rectify(dst, bank_cols, e, nb):
+            nc.scalar.activation(out=dst, in_=bank_cols, func=ACT.Relu, bias=bias[:, nb, e:e + 1])
 
         starts = [sum(CHUNKS[:c]) for c in range(len(CHUNKS))]
         last = len(CHUNKS) - 1
+        picked = {}
         woven = {}
 
+        def entries(c):
+            return offs_sb[:, starts[c] // 16:(starts[c] + CHUNKS[c]) // 16]
+
+        def new_woven(c):
+            woven[c] = keep.tile([P, CHUNKS[c] * 2], U32, name=f"woven{c}", tag=WOVEN_TAGS[c], align_bytes=64)
+            return woven[c][:].rearrange("p (n g) -> p n g", g=2)
+
         def gather(c):
-            width = CHUNKS[c]
-            entries = offs_sb[:, starts[c] // 16:(starts[c] + width) // 16]
-            woven[c] = keep.tile([P, width * 2], U32, name=f"woven{c}", tag=f"stage{c - 2 if c == last else c}", align_bytes=64)
-            side_by_side = woven[c][:].rearrange("p (n g) -> p n g", g=2)
             if c == last:
+                side_by_side = new_woven(c)
                 for g in range(2):
-                    nc.vector.tensor_copy(out=side_by_side[:, :, g], in_=pairs[g][:].bitcast(U32).indirect(entries))
+                    nc.vector.tensor_copy(out=side_by_side[:, :, g], in_=pairs[g][:].bitcast(U32).indirect(entries(c)))
                 return
-            picked = keep.tile([P, 2, width], U32, name=f"picked{c}", tag=f"stage{c - 2}", align_bytes=64)
+            picked[c] = keep.tile([P, 2, CHUNKS[c]], U32, name=f"picked{c}", tag=PICKED_TAGS[c], align_bytes=64)
             for g in range(2):
-                nc.vector.tensor_copy(out=picked[:, g, :], in_=pairs[g][:].bitcast(U32).indirect(entries))
-            nc.scalar.copy(out=side_by_side, in_=picked[:].rearrange("p g n -> p n g"))
+                nc.vector.tensor_copy(out=picked[c][:, g, :], in_=pairs[g][:].bitcast(U32).indirect(entries(c)))
+
+        def weave(c):
+            nc.scalar.copy(out=new_woven(c), in_=picked[c][:].rearrange("p g n -> p n g"))
 
         def multiply(c):
             width = CHUNKS[c]
-            codes, scales = quantise(woven[c][:].bitcast(BF16), width, f"x{c}")
-            bank = psum.tile([P, width], F32, name=f"y0_bank{c}", tag="x_bank00" if c == last else f"y0_bank{c}")
+            codes, scales = quantise(woven[c][:].bitcast(BF16), width, f"x{c}", "chain3" if c == last else None)
+            bank = psum.tile([P, width], F32, name=f"y0_bank{c}", tag=Y0_BANKS[c])
             for i in range(width // C):
                 slot_q.append((codes, scales, i * C))
                 expert(bank[:, i * C:(i + 1) * C], starts[c] // C + i, 0)
             return bank
 
         def finish(c, bank):
+            relu = keep.tile([P, CHUNKS[c]], F32, name=f"relu0{c}", tag=RELU_TAGS[c], align_bytes=64)
             for i in range(CHUNKS[c] // C):
-                rectify(bank[:, i * C:(i + 1) * C], starts[c] // C + i, 0)
-            square(0, starts[c], starts[c] + CHUNKS[c])
+                rectify(relu[:, i * C:(i + 1) * C], bank[:, i * C:(i + 1) * C], starts[c] // C + i, 0)
+            nc.scalar.activation(out=y[0][:, starts[c]:starts[c] + CHUNKS[c]], in_=relu[:], func=ACT.Square)
 
-        gather(0)
-        gather(1)
-        for c in range(len(CHUNKS)):
+        for c in range(2):
+            gather(c)
+            weave(c)
+        for c in range(last - 1):
             bank = multiply(c)
-            if c + 2 <= last:
-                gather(c + 2)
+            gather(c + 2)
+            if c + 2 < last:
+                weave(c + 2)
             finish(c, bank)
+        banks = [multiply(c) for c in (last - 1, last)]
+        relu = keep.tile([P, 2 * C], F32, name="relu_last", tag="chain2", align_bytes=64)
+        for i in range(2):
+            e = E - 2 + i
+            nc.vector.tensor_scalar(relu[:, i * C:(i + 1) * C], banks[i][:], bias[:, 0, e:e + 1], 0.0, ALU.add, ALU.max)
+        nc.vector.tensor_tensor(y[0][:, S - 2 * C:], relu[:], relu[:], ALU.mult)
 
-        for q in (1, 0):
-            bank = psum.tile([P, 4 * C], F32, name=f"y1_bank{q}", tag="x_bank01" if q == 1 else f"y0_bank{last - 1}")
+        late = keep.tile([P, S], F32, name="relu1", tag="relu02", align_bytes=64)
+        for q in range(2):
+            bank = psum.tile([P, 4 * C], F32, name=f"y1_bank{q}", tag=("x_bank0_384", "x_bank1_256")[q])
             for i in range(4):
                 expert(bank[:, i * C:(i + 1) * C], 4 * q + i, 1)
             for i in range(4):
-                rectify(bank[:, i * C:(i + 1) * C], 4 * q + i, 1)
-            square(1, q * 4 * C, (q + 1) * 4 * C)
+                cols = slice(i * C, (i + 1) * C)
+                e = 4 * q + i
+                rectify(late[:, e * C:(e + 1) * C], bank[:, cols], e, 1)
+            cols = slice(q * 4 * C, (q + 1) * 4 * C)
+            nc.scalar.activation(out=y[1][:, cols], in_=late[:, cols], func=ACT.Square)
 
-        for nb in range(2):
-            terms = keep.tile([P, 2, T], F32, name=f"terms{nb}")
-            for r in range(2):
-                nc.vector.tensor_tensor(terms[:, r, :], y[nb][:].indirect(pos_sb[r][:]), gate_sb[:, r, :], ALU.mult)
-            total = keep.tile([P, T], F32, name=f"total{nb}")
-            nc.vector.tensor_tensor(total[:], terms[:, 0, :], terms[:, 1, :], ALU.add)
-            nc.sync.dma_start(out=out[nb * P:(nb + 1) * P, :], in_=total[:])
+        def gated_turned(nb, r, tag):
+            picked = keep.tile([P, T], F32, name=f"y_picked{nb}{r}")
+            nc.vector.tensor_copy(out=picked[:], in_=y[nb][:].indirect(pos_sb[r][:]))
+            bank = psum.tile([P, T], F32, name=f"turned{nb}{r}", tag=tag)
+            for i in range(4):
+                nc.tensor.transpose(bank[:, i * P:(i + 1) * P], picked[:, i * P:(i + 1) * P], ident[:])
+            scaled = keep.tile([P, T], F32, name=f"scaled{nb}{r}")
+            for i in range(4):
+                nc.scalar.activation(
+                    out=scaled[:, i * P:(i + 1) * P], in_=bank[:, i * P:(i + 1) * P], func=ACT.Copy,
+                    scale=gate_cols[:, r, i:i + 1],
+                )
+            return scaled
+
+        terms0 = [gated_turned(0, 0, "spare0"), gated_turned(0, 1, "spare1")]
+        total0 = keep.tile([P, T], F32, name="total0")
+        for h, tag in enumerate(("x_bank1_0", "x_bank1_384")):
+            bank = psum.tile([P, HALF], F32, name=f"sum0{h}", tag=tag)
+            for i in range(2):
+                for r in range(2):
+                    cols = slice(h * HALF + i * P, h * HALF + (i + 1) * P)
+                    nc.tensor.matmul(
+                        bank[:, i * P:(i + 1) * P], terms0[r][:, cols], ident[:],
+                        start=(r == 0), stop=(r == 1), is_transpose=True,
+                    )
+            nc.scalar.copy(out=total0[:, h * HALF:(h + 1) * HALF], in_=bank[:])
+        nc.sync.dma_start(out=out[0:P, :], in_=total0[:])
+        terms1 = keep.tile([P, 2, T], F32, name="terms1")
+        for r in range(2):
+            nc.vector.tensor_tensor(terms1[:, r, :], y[1][:].indirect(pos_sb[r][:]), gate_rows[:, r, :], ALU.mult)
+        total1 = keep.tile([P, T], F32, name="total1")
+        nc.vector.tensor_tensor(total1[:], terms1[:, 0, :], terms1[:, 1, :], ALU.add)
+        nc.sync.dma_start(out=out[P:2 * P, :], in_=total1[:])

@@ -25,10 +25,12 @@ PASS = P * PACK
 HALF = T // 2
 U_VECTOR = 128
 W_VECTOR = 64
+U_PIECES = ((0, 0, 256), (1, 0, 256), (0, 256, 256), (1, 256, 128), (1, 384, 128))
 CHUNKS = (256, 256, 256, 128, 128)
 WOVEN_TAGS = ("chain0", "chain1", "chain2", "chain3", "chain2")
 PICKED_TAGS = ("picked0", "picked1", "chain0", "chain1")
 RELU_TAGS = ("relu00", "relu01", "relu02")
+SUM_BANKS = ("spare0", "spare1", "x_bank0_0", "x_bank1_0")
 Y0_BANKS = ("spare0", "spare1", "x_bank0_0", "x_bank1_0", "x_bank0_256")
 
 
@@ -46,14 +48,12 @@ def tile_moe_prv_lin_relu2_kernel(
             nc.sync.dma_start(out=raw[:], in_=wu[a * PASS:(a + 1) * PASS, :].rearrange("(p j) c -> p j c", j=PACK))
             wu_raw.append(raw)
         u_raw = {}
-        for h in range(2):
-            for a in range(2):
-                raw = keep.tile([P, PACK, HALF], F32, name=f"u_raw{h}{a}")
-                nc.sync.dma_start(
-                    out=raw[:],
-                    in_=uT[a * PASS:(a + 1) * PASS, h * HALF:(h + 1) * HALF].rearrange("(p j) c -> p j c", j=PACK),
-                )
-                u_raw[h, a] = raw
+        for a, t0, width in U_PIECES:
+            raw = keep.tile([P, PACK, width], F32, name=f"u_raw{a}_{t0}")
+            nc.sync.dma_start(
+                out=raw[:], in_=uT[a * PASS:(a + 1) * PASS, t0:t0 + width].rearrange("(p j) c -> p j c", j=PACK)
+            )
+            u_raw[a, t0] = raw
         offs_sb = keep.tile([P, S // 16], U16, name="offs_sb")
         nc.sync.dma_start(offs_sb[:], offs)
         ww = keep.tile([P, E * 2 * N], U8, name="ww", align_bytes=64)
@@ -68,10 +68,6 @@ def tile_moe_prv_lin_relu2_kernel(
             nc.sync.dma_start(out=ws[r:P:32, :].bitcast(I32).rearrange("q (e n) -> q e n", e=E), in_=rows[r])
         bias = keep.tile([P, 2, E], F32, name="bias")
         nc.sync.dma_start(out=bias[:], in_=b.rearrange("(h p) e -> p h e", p=P))
-        gate_cols = keep.tile([P, 2, 8], F32, name="gate_cols")
-        with nc.allow_non_contiguous_dma(reason="one gate value a token, a token a partition"):
-            for r in range(2):
-                nc.sync.dma_start(out=gate_cols[:, r, 0:4], in_=gate[r, N - 1, :].rearrange("(i p) -> p i", p=P))
         gate_rows = keep.tile([P, 2, T], F32, name="gate_rows")
         nc.sync.dma_start(out=gate_rows[:], in_=gate[:, 0:P, :].rearrange("r p t -> p r t"))
         ident = keep.tile([P, P], F32, name="ident")
@@ -99,17 +95,18 @@ def tile_moe_prv_lin_relu2_kernel(
 
         pairs = [keep.tile([P, T * 2], BF16, name=f"pairs{g}", align_bytes=64) for g in range(2)]
 
-        def interleave(h, a, name, t0, t1, split):
-            grouped = keep.tile([P, (t1 - t0) * PACK], BF16, name=f"{name}_grouped", align_bytes=64)
+        u_q = {}
+
+        def prepare(a, t0, width):
+            grouped = keep.tile([P, width * PACK], BF16, name=f"u_grouped{a}_{t0}", align_bytes=64)
             dst = grouped[:].rearrange("p (c i j) -> p c j i", i=4, j=PACK)
-            src = u_raw[h, a][:, :, t0:t1].rearrange("p j (c i) -> p c j i", i=4)
-            if split:
-                cut = U_VECTOR // 4
-                nc.vector.tensor_copy(out=dst[:, :cut], in_=src[:, :cut])
+            src = u_raw[a, t0][:].rearrange("p j (c i) -> p c j i", i=4)
+            cut = U_VECTOR // 4
+            nc.vector.tensor_copy(out=dst[:, :cut], in_=src[:, :cut])
+            if width > U_VECTOR:
                 nc.scalar.copy(out=dst[:, cut:], in_=src[:, cut:])
-            else:
-                nc.vector.tensor_copy(out=dst, in_=src)
-            return grouped
+            codes, scales = quantise(grouped[:], width, f"u{a}_{t0}")
+            u_q[a, t0] = (codes, scales)
 
         def project(bank, g, j, a, operand):
             codes, scales = operand
@@ -134,25 +131,24 @@ def tile_moe_prv_lin_relu2_kernel(
                 for t0, width, operands in groups:
                     for j, a in ((0, 1), (1, 0), (1, 1)):
                         project(banks[g, t0], g, j, a, operands[a])
-                    nc.scalar.copy(
-                        out=pairs[g][:, 2 * t0:2 * (t0 + width)].rearrange("p (n j) -> p n j", j=2),
-                        in_=banks[g, t0][:].rearrange("p j n -> p n j"),
-                    )
+                    dst = pairs[g][:, 2 * t0:2 * (t0 + width)].rearrange("p (n j) -> p n j", j=2)
+                    src = banks[g, t0][:].rearrange("p j n -> p n j")
+                    if t0 == HALF:
+                        nc.vector.tensor_copy(out=dst, in_=src)
+                    else:
+                        nc.scalar.copy(out=dst, in_=src)
 
-        first = []
-        for a in range(2):
-            codes, scales = quantise(interleave(0, a, f"u0{a}", 0, HALF, True)[:], HALF, f"u0{a}")
-            first.append((codes[:], scales[:]))
-        project_tokens([(0, HALF, first)])
-        codes0, scales0 = quantise(interleave(1, 0, "u10", 0, HALF, True)[:], HALF, "u10")
-        staged = [interleave(1, 1, f"u11{i}", i * P, (i + 1) * P, False) for i in range(2)]
+        for piece in U_PIECES[:2]:
+            prepare(*piece)
+        project_tokens([(0, HALF, [(u_q[a, 0][0][:], u_q[a, 0][1][:]) for a in range(2)])])
+        for piece in U_PIECES[2:]:
+            prepare(*piece)
         groups = []
         for i in range(2):
-            codes, scales = quantise(staged[i][:], P, f"u11{i}")
             cols = slice(i * P, (i + 1) * P)
-            groups.append((HALF + i * P, P, [(codes0[:, cols], scales0[:, cols]), (codes[:], scales[:])]))
+            early, final = u_q[0, HALF], u_q[1, HALF + i * P]
+            groups.append((HALF + i * P, P, [(early[0][:, cols], early[1][:, cols]), (final[0][:], final[1][:])]))
         project_tokens(groups)
-
 
         y = [keep.tile([P, S], F32, name=f"y{nb}") for nb in range(2)]
         slot_q = []
@@ -226,8 +222,9 @@ def tile_moe_prv_lin_relu2_kernel(
         relu = keep.tile([P, 2 * C], F32, name="relu_last", tag="chain2", align_bytes=64)
         for i in range(2):
             e = E - 2 + i
-            nc.vector.tensor_scalar(relu[:, i * C:(i + 1) * C], banks[i][:], bias[:, 0, e:e + 1], 0.0, ALU.add, ALU.max)
-        nc.vector.tensor_tensor(y[0][:, S - 2 * C:], relu[:], relu[:], ALU.mult)
+            cols = slice(i * C, (i + 1) * C)
+            nc.vector.tensor_scalar(relu[:, cols], banks[i][:], bias[:, 0, e:e + 1], 0.0, ALU.add, ALU.max)
+            nc.vector.tensor_tensor(y[0][:, e * C:(e + 1) * C], relu[:, cols], relu[:, cols], ALU.mult)
 
         late = keep.tile([P, S], F32, name="relu1", tag="relu02", align_bytes=64)
         for q in range(2):
@@ -241,36 +238,34 @@ def tile_moe_prv_lin_relu2_kernel(
             cols = slice(q * 4 * C, (q + 1) * 4 * C)
             nc.scalar.activation(out=y[1][:, cols], in_=late[:, cols], func=ACT.Square)
 
-        def gated_turned(nb, r, tag):
-            picked = keep.tile([P, T], F32, name=f"y_picked{nb}{r}")
-            nc.vector.tensor_copy(out=picked[:], in_=y[nb][:].indirect(pos_sb[r][:]))
-            bank = psum.tile([P, T], F32, name=f"turned{nb}{r}", tag=tag)
-            for i in range(4):
-                nc.tensor.transpose(bank[:, i * P:(i + 1) * P], picked[:, i * P:(i + 1) * P], ident[:])
-            scaled = keep.tile([P, T], F32, name=f"scaled{nb}{r}")
-            for i in range(4):
-                nc.scalar.activation(
-                    out=scaled[:, i * P:(i + 1) * P], in_=bank[:, i * P:(i + 1) * P], func=ACT.Copy,
-                    scale=gate_cols[:, r, i:i + 1],
-                )
-            return scaled
+        terms = [keep.tile([P, 2, T], F32, name=f"terms{nb}") for nb in range(2)]
 
-        terms0 = [gated_turned(0, 0, "spare0"), gated_turned(0, 1, "spare1")]
+        def gated(nb, r):
+            nc.vector.tensor_tensor(terms[nb][:, r, :], y[nb][:].indirect(pos_sb[r][:]), gate_rows[:, r, :], ALU.mult)
+
+        sums = [psum.tile([P, P], F32, name=f"turned_sum{i}", tag=SUM_BANKS[i]) for i in range(4)]
+        for r in range(2):
+            gated(0, r)
+            for i in range(4):
+                nc.tensor.matmul(
+                    sums[i][:], terms[0][:, r, i * P:(i + 1) * P], ident[:],
+                    start=(r == 0), stop=(r == 1), is_transpose=True,
+                )
+        turned = keep.tile([P, T], F32, name="turned", tag="relu02", align_bytes=64)
+        for i in range(4):
+            nc.scalar.copy(out=turned[:, i * P:(i + 1) * P], in_=sums[i][:])
         total0 = keep.tile([P, T], F32, name="total0")
-        for h, tag in enumerate(("x_bank1_0", "x_bank1_384")):
+        for h, tag in enumerate(("x_bank0_256", "x_bank1_384")):
             bank = psum.tile([P, HALF], F32, name=f"sum0{h}", tag=tag)
             for i in range(2):
-                for r in range(2):
-                    cols = slice(h * HALF + i * P, h * HALF + (i + 1) * P)
-                    nc.tensor.matmul(
-                        bank[:, i * P:(i + 1) * P], terms0[r][:, cols], ident[:],
-                        start=(r == 0), stop=(r == 1), is_transpose=True,
-                    )
+                cols = slice(h * HALF + i * P, h * HALF + (i + 1) * P)
+                nc.tensor.transpose(bank[:, i * P:(i + 1) * P], turned[:, cols], ident[:])
             nc.scalar.copy(out=total0[:, h * HALF:(h + 1) * HALF], in_=bank[:])
         nc.sync.dma_start(out=out[0:P, :], in_=total0[:])
-        terms1 = keep.tile([P, 2, T], F32, name="terms1")
         for r in range(2):
-            nc.vector.tensor_tensor(terms1[:, r, :], y[1][:].indirect(pos_sb[r][:]), gate_rows[:, r, :], ALU.mult)
+            gated(1, r)
         total1 = keep.tile([P, T], F32, name="total1")
-        nc.vector.tensor_tensor(total1[:], terms1[:, 0, :], terms1[:, 1, :], ALU.add)
-        nc.sync.dma_start(out=out[P:2 * P, :], in_=total1[:])
+        for h in range(2):
+            cols = slice(h * HALF, (h + 1) * HALF)
+            nc.vector.tensor_tensor(total1[:, cols], terms[1][:, 0, cols], terms[1][:, 1, cols], ALU.add)
+            nc.sync.dma_start(out=out[P:2 * P, cols], in_=total1[:, cols])

@@ -22,16 +22,23 @@ ALU = mybir.AluOpType
 P = 128
 PACK = 4
 PASS = P * PACK
+PASSES = F // PASS
 HALF = T // 2
+PER_COLUMN = 16
+BLOCKS = T // P
+BANK_EXPERTS = 4
+
+U_PIECES = ((0, 0, HALF), (1, 0, HALF), (0, HALF, HALF), (1, HALF, P), (1, HALF + P, P))
 U_VECTOR = 128
-W_VECTOR = 64
-U_PIECES = ((0, 0, 256), (1, 0, 256), (0, 256, 256), (1, 256, 128), (1, 384, 128))
 CHUNKS = (256, 256, 256, 128, 128)
+
 WOVEN_TAGS = ("chain0", "chain1", "chain2", "chain3", "chain2")
 PICKED_TAGS = ("picked0", "picked1", "chain0", "chain1")
 RELU_TAGS = ("relu00", "relu01", "relu02")
-SUM_BANKS = ("spare0", "spare1", "x_bank0_0", "x_bank1_0")
 Y0_BANKS = ("spare0", "spare1", "x_bank0_0", "x_bank1_0", "x_bank0_256")
+Y1_BANKS = ("x_bank0_384", "x_bank1_256")
+SUM_BANKS = ("spare0", "spare1", "x_bank0_0", "x_bank1_0")
+BACK_BANKS = ("x_bank0_256", "x_bank1_384")
 
 
 def tile_moe_prv_lin_relu2_kernel(
@@ -43,7 +50,7 @@ def tile_moe_prv_lin_relu2_kernel(
         psum = ctx.enter_context(tc.psum_pool(name="psum", bufs=1))
 
         wu_raw = []
-        for a in range(2):
+        for a in range(PASSES):
             raw = keep.tile([P, PACK, K], F32, name=f"wu_raw{a}")
             nc.sync.dma_start(out=raw[:], in_=wu[a * PASS:(a + 1) * PASS, :].rearrange("(p j) c -> p j c", j=PACK))
             wu_raw.append(raw)
@@ -54,8 +61,9 @@ def tile_moe_prv_lin_relu2_kernel(
                 out=raw[:], in_=uT[a * PASS:(a + 1) * PASS, t0:t0 + width].rearrange("(p j) c -> p j c", j=PACK)
             )
             u_raw[a, t0] = raw
-        offs_sb = keep.tile([P, S // 16], U16, name="offs_sb")
+        offs_sb = keep.tile([P, S // PER_COLUMN], U16, name="offs_sb")
         nc.sync.dma_start(offs_sb[:], offs)
+
         ww = keep.tile([P, E * 2 * N], U8, name="ww", align_bytes=64)
         nc.sync.dma_start(
             out=ww[:].bitcast(I32).rearrange("p (e n) -> p e n", e=E),
@@ -63,9 +71,9 @@ def tile_moe_prv_lin_relu2_kernel(
         )
         ws = keep.tile([P, E * N], U8, name="ws", align_bytes=64)
         nc.gpsimd.memset(ws[:].bitcast(I32), 0)
-        rows = w_scales.bitcast(I32).rearrange("e a (q r) n -> r q (e a) n", r=4)
+        scale_rows = w_scales.bitcast(I32).rearrange("e a (q r) n -> r q (e a) n", r=4)
         for r in range(4):
-            nc.sync.dma_start(out=ws[r:P:32, :].bitcast(I32).rearrange("q (e n) -> q e n", e=E), in_=rows[r])
+            nc.sync.dma_start(out=ws[r:P:32, :].bitcast(I32).rearrange("q (e n) -> q e n", e=E), in_=scale_rows[r])
         bias = keep.tile([P, 2, E], F32, name="bias")
         nc.sync.dma_start(out=bias[:], in_=b.rearrange("(h p) e -> p h e", p=P))
         gate_rows = keep.tile([P, 2, T], F32, name="gate_rows")
@@ -74,27 +82,26 @@ def tile_moe_prv_lin_relu2_kernel(
         make_identity(nc, ident[:])
         pos_sb = []
         for r, pos in enumerate((pos1, pos2)):
-            lst = keep.tile([P, T // 16], U16, name=f"pos_sb{r}")
-            nc.sync.dma_start(lst[:], pos)
-            pos_sb.append(lst)
+            positions = keep.tile([P, T // PER_COLUMN], U16, name=f"pos_sb{r}")
+            nc.sync.dma_start(positions[:], pos)
+            pos_sb.append(positions)
 
-        def quantise(grouped, width, name, tag=None):
+        def quantise(values, width, name, tag=None):
             codes = keep.tile([P, width], U32, name=f"{name}_codes", tag=tag or f"{name}_codes", align_bytes=64)
             scales = keep.tile([P, width], U8, name=f"{name}_scales", align_bytes=64)
-            nc.vector.quantize_mx(out=codes[:].bitcast(FP8X4), scales=scales[:], in_=grouped)
+            nc.vector.quantize_mx(out=codes[:].bitcast(FP8X4), scales=scales[:], in_=values)
             return codes, scales
 
         wu_q = []
-        for a in range(2):
+        for a in range(PASSES):
             grouped = keep.tile([P, K * PACK], BF16, name=f"wu_grouped{a}", align_bytes=64)
             dst = grouped[:].rearrange("p (t m j) -> p m j t", t=PACK, j=PACK)
             src = wu_raw[a][:].rearrange("p j (m t) -> p m j t", t=PACK)
-            nc.vector.tensor_copy(out=dst[:, :W_VECTOR], in_=src[:, :W_VECTOR])
-            nc.scalar.copy(out=dst[:, W_VECTOR:], in_=src[:, W_VECTOR:])
+            nc.vector.tensor_copy(out=dst[:, :, :, :2], in_=src[:, :, :, :2])
+            nc.scalar.copy(out=dst[:, :, :, 2:], in_=src[:, :, :, 2:])
             wu_q.append(quantise(grouped[:], K, f"wu{a}"))
 
         pairs = [keep.tile([P, T * 2], BF16, name=f"pairs{g}", align_bytes=64) for g in range(2)]
-
         u_q = {}
 
         def prepare(a, t0, width):
@@ -105,8 +112,7 @@ def tile_moe_prv_lin_relu2_kernel(
             nc.vector.tensor_copy(out=dst[:, :cut], in_=src[:, :cut])
             if width > U_VECTOR:
                 nc.scalar.copy(out=dst[:, cut:], in_=src[:, cut:])
-            codes, scales = quantise(grouped[:], width, f"u{a}_{t0}")
-            u_q[a, t0] = (codes, scales)
+            u_q[a, t0] = quantise(grouped[:], width, f"u{a}_{t0}")
 
         def project(bank, g, j, a, operand):
             codes, scales = operand
@@ -118,37 +124,37 @@ def tile_moe_prv_lin_relu2_kernel(
                 rhs=codes.bitcast(FP8X4),
                 rhs_scale=scales,
                 start=(a == 0),
-                stop=(a == 1),
+                stop=(a == PASSES - 1),
             )
 
         def project_tokens(groups):
-            banks = {}
+            x_banks = {}
             for g in range(2):
                 for t0, width, operands in groups:
-                    banks[g, t0] = psum.tile([P, 2, width], F32, name=f"x_bank{g}_{t0}")
-                    project(banks[g, t0], g, 0, 0, operands[0])
+                    x_banks[g, t0] = psum.tile([P, 2, width], F32, name=f"x_bank{g}_{t0}")
+                    project(x_banks[g, t0], g, 0, 0, operands[0])
             for g in range(2):
                 for t0, width, operands in groups:
                     for j, a in ((0, 1), (1, 0), (1, 1)):
-                        project(banks[g, t0], g, j, a, operands[a])
+                        project(x_banks[g, t0], g, j, a, operands[a])
                     dst = pairs[g][:, 2 * t0:2 * (t0 + width)].rearrange("p (n j) -> p n j", j=2)
-                    src = banks[g, t0][:].rearrange("p j n -> p n j")
+                    src = x_banks[g, t0][:].rearrange("p j n -> p n j")
                     if t0 == HALF:
                         nc.vector.tensor_copy(out=dst, in_=src)
                     else:
                         nc.scalar.copy(out=dst, in_=src)
 
-        for piece in U_PIECES[:2]:
+        for piece in U_PIECES[:PASSES]:
             prepare(*piece)
-        project_tokens([(0, HALF, [(u_q[a, 0][0][:], u_q[a, 0][1][:]) for a in range(2)])])
-        for piece in U_PIECES[2:]:
+        project_tokens([(0, HALF, [(u_q[a, 0][0][:], u_q[a, 0][1][:]) for a in range(PASSES)])])
+        for piece in U_PIECES[PASSES:]:
             prepare(*piece)
-        groups = []
+        quarters = []
         for i in range(2):
             cols = slice(i * P, (i + 1) * P)
             early, final = u_q[0, HALF], u_q[1, HALF + i * P]
-            groups.append((HALF + i * P, P, [(early[0][:, cols], early[1][:, cols]), (final[0][:], final[1][:])]))
-        project_tokens(groups)
+            quarters.append((HALF + i * P, P, [(early[0][:, cols], early[1][:, cols]), (final[0][:], final[1][:])]))
+        project_tokens(quarters)
 
         y = [keep.tile([P, S], F32, name=f"y{nb}") for nb in range(2)]
         slot_q = []
@@ -175,7 +181,7 @@ def tile_moe_prv_lin_relu2_kernel(
         woven = {}
 
         def entries(c):
-            return offs_sb[:, starts[c] // 16:(starts[c] + CHUNKS[c]) // 16]
+            return offs_sb[:, starts[c] // PER_COLUMN:(starts[c] + CHUNKS[c]) // PER_COLUMN]
 
         def new_woven(c):
             woven[c] = keep.tile([P, CHUNKS[c] * 2], U32, name=f"woven{c}", tag=WOVEN_TAGS[c], align_bytes=64)
@@ -213,55 +219,55 @@ def tile_moe_prv_lin_relu2_kernel(
             gather(c)
             weave(c)
         for c in range(last - 1):
-            bank = multiply(c)
+            chunk_bank = multiply(c)
             gather(c + 2)
             if c + 2 < last:
                 weave(c + 2)
-            finish(c, bank)
-        banks = [multiply(c) for c in (last - 1, last)]
-        relu = keep.tile([P, 2 * C], F32, name="relu_last", tag="chain2", align_bytes=64)
+            finish(c, chunk_bank)
+        last_banks = [multiply(c) for c in (last - 1, last)]
+        relu_last = keep.tile([P, 2 * C], F32, name="relu_last", tag="chain2", align_bytes=64)
         for i in range(2):
             e = E - 2 + i
             cols = slice(i * C, (i + 1) * C)
-            nc.vector.tensor_scalar(relu[:, cols], banks[i][:], bias[:, 0, e:e + 1], 0.0, ALU.add, ALU.max)
-            nc.vector.tensor_tensor(y[0][:, e * C:(e + 1) * C], relu[:, cols], relu[:, cols], ALU.mult)
+            nc.vector.tensor_scalar(relu_last[:, cols], last_banks[i][:], bias[:, 0, e:e + 1], 0.0, ALU.add, ALU.max)
+            nc.vector.tensor_tensor(y[0][:, e * C:(e + 1) * C], relu_last[:, cols], relu_last[:, cols], ALU.mult)
 
-        late = keep.tile([P, S], F32, name="relu1", tag="relu02", align_bytes=64)
-        for q in range(2):
-            bank = psum.tile([P, 4 * C], F32, name=f"y1_bank{q}", tag=("x_bank0_384", "x_bank1_256")[q])
-            for i in range(4):
-                expert(bank[:, i * C:(i + 1) * C], 4 * q + i, 1)
-            for i in range(4):
-                cols = slice(i * C, (i + 1) * C)
-                e = 4 * q + i
-                rectify(late[:, e * C:(e + 1) * C], bank[:, cols], e, 1)
-            cols = slice(q * 4 * C, (q + 1) * 4 * C)
-            nc.scalar.activation(out=y[1][:, cols], in_=late[:, cols], func=ACT.Square)
+        relu1 = keep.tile([P, S], F32, name="relu1", tag="relu02", align_bytes=64)
+        for q, tag in enumerate(Y1_BANKS):
+            y1_bank = psum.tile([P, BANK_EXPERTS * C], F32, name=f"y1_bank{q}", tag=tag)
+            for i in range(BANK_EXPERTS):
+                expert(y1_bank[:, i * C:(i + 1) * C], BANK_EXPERTS * q + i, 1)
+            for i in range(BANK_EXPERTS):
+                e = BANK_EXPERTS * q + i
+                rectify(relu1[:, e * C:(e + 1) * C], y1_bank[:, i * C:(i + 1) * C], e, 1)
+            cols = slice(q * BANK_EXPERTS * C, (q + 1) * BANK_EXPERTS * C)
+            nc.scalar.activation(out=y[1][:, cols], in_=relu1[:, cols], func=ACT.Square)
 
         terms = [keep.tile([P, 2, T], F32, name=f"terms{nb}") for nb in range(2)]
 
         def gated(nb, r):
             nc.vector.tensor_tensor(terms[nb][:, r, :], y[nb][:].indirect(pos_sb[r][:]), gate_rows[:, r, :], ALU.mult)
 
-        sums = [psum.tile([P, P], F32, name=f"turned_sum{i}", tag=SUM_BANKS[i]) for i in range(4)]
+        sum_banks = [psum.tile([P, P], F32, name=f"turned_sum{i}", tag=SUM_BANKS[i]) for i in range(BLOCKS)]
         for r in range(2):
             gated(0, r)
-            for i in range(4):
+            for i in range(BLOCKS):
                 nc.tensor.matmul(
-                    sums[i][:], terms[0][:, r, i * P:(i + 1) * P], ident[:],
+                    sum_banks[i][:], terms[0][:, r, i * P:(i + 1) * P], ident[:],
                     start=(r == 0), stop=(r == 1), is_transpose=True,
                 )
         turned = keep.tile([P, T], F32, name="turned", tag="relu02", align_bytes=64)
-        for i in range(4):
-            nc.scalar.copy(out=turned[:, i * P:(i + 1) * P], in_=sums[i][:])
+        for i in range(BLOCKS):
+            nc.scalar.copy(out=turned[:, i * P:(i + 1) * P], in_=sum_banks[i][:])
         total0 = keep.tile([P, T], F32, name="total0")
-        for h, tag in enumerate(("x_bank0_256", "x_bank1_384")):
-            bank = psum.tile([P, HALF], F32, name=f"sum0{h}", tag=tag)
+        for h, tag in enumerate(BACK_BANKS):
+            back_bank = psum.tile([P, HALF], F32, name=f"sum0{h}", tag=tag)
             for i in range(2):
                 cols = slice(h * HALF + i * P, h * HALF + (i + 1) * P)
-                nc.tensor.transpose(bank[:, i * P:(i + 1) * P], turned[:, cols], ident[:])
-            nc.scalar.copy(out=total0[:, h * HALF:(h + 1) * HALF], in_=bank[:])
+                nc.tensor.transpose(back_bank[:, i * P:(i + 1) * P], turned[:, cols], ident[:])
+            nc.scalar.copy(out=total0[:, h * HALF:(h + 1) * HALF], in_=back_bank[:])
         nc.sync.dma_start(out=out[0:P, :], in_=total0[:])
+
         for r in range(2):
             gated(1, r)
         total1 = keep.tile([P, T], F32, name="total1")

from contextlib import ExitStack

import concourse.mybir as mybir
from concourse.masks import make_identity

F, K, T, E, C, N = 1024, 512, 512, 8, 128, 256
S = E * C

FLOPS = 2 * F * K * T + 2 * K * N * S

F32 = mybir.dt.float32
BF16 = mybir.dt.bfloat16
I32 = mybir.dt.int32
U32 = mybir.dt.uint32
U16 = mybir.dt.uint16
U8 = mybir.dt.uint8
FP8X4 = mybir.dt.float8_e4m3fn_x4
FP4X4 = mybir.dt.float4_e2m1fn_x4
ACT = mybir.ActivationFunctionType
ALU = mybir.AluOpType

P = 128
PACK = 4
PASS = P * PACK
PASSES = F // PASS
HALF = T // 2
PER_COLUMN = 16
BLOCKS = T // P
BANK_EXPERTS = 4

U_PIECES = ((0, 0, HALF), (1, 0, HALF), (0, HALF, HALF), (1, HALF, P), (1, HALF + P, P))
U_VECTOR = 128
CHUNKS = (256, 256, 256, 128, 128)

WOVEN_TAGS = ("chain0", "chain1", "chain2", "chain3", "chain2")
PICKED_TAGS = ("picked0", "picked1", "chain0", "chain1")
RELU_TAGS = ("relu00", "relu01", "relu02")
Y0_BANKS = ("spare0", "spare1", "x_bank0_0", "x_bank1_0", "x_bank0_256")
Y1_BANKS = ("x_bank0_384", "x_bank1_256")
SUM_BANKS = ("spare0", "spare1", "x_bank0_0", "x_bank1_0")
BACK_BANKS = ("x_bank0_256", "x_bank1_384")


def tile_moe_prv_lin_relu2_kernel(
    tc, uT, wu, w_words, w_scales, b, gate, offs, pos1, pos2, out
):
    nc = tc.nc
    with ExitStack() as ctx:
        keep = ctx.enter_context(tc.tile_pool(name="keep", bufs=1))
        psum = ctx.enter_context(tc.psum_pool(name="psum", bufs=1))

        wu_raw = []
        for a in range(PASSES):
            raw = keep.tile([P, PACK, K], F32, name=f"wu_raw{a}")
            nc.sync.dma_start(out=raw[:], in_=wu[a * PASS:(a + 1) * PASS, :].rearrange("(p j) c -> p j c", j=PACK))
            wu_raw.append(raw)
        u_raw = {}
        for a, t0, width in U_PIECES:
            raw = keep.tile([P, PACK, width], F32, name=f"u_raw{a}_{t0}")
            nc.sync.dma_start(
                out=raw[:], in_=uT[a * PASS:(a + 1) * PASS, t0:t0 + width].rearrange("(p j) c -> p j c", j=PACK)
            )
            u_raw[a, t0] = raw
        offs_sb = keep.tile([P, S // PER_COLUMN], U16, name="offs_sb")
        nc.sync.dma_start(offs_sb[:], offs)

        ww = keep.tile([P, E * 2 * N], U8, name="ww", align_bytes=64)
        nc.sync.dma_start(
            out=ww[:].bitcast(I32).rearrange("p (e n) -> p e n", e=E),
            in_=w_words.bitcast(I32).rearrange("e a p n -> p (e a) n"),
        )
        ws = keep.tile([P, E * N], U8, name="ws", align_bytes=64)
        nc.gpsimd.memset(ws[:].bitcast(I32), 0)
        scale_rows = w_scales.bitcast(I32).rearrange("e a (q r) n -> r q (e a) n", r=4)
        for r in range(4):
            nc.sync.dma_start(out=ws[r:P:32, :].bitcast(I32).rearrange("q (e n) -> q e n", e=E), in_=scale_rows[r])
        bias = keep.tile([P, 2, E], F32, name="bias")
        nc.sync.dma_start(out=bias[:], in_=b.rearrange("(h p) e -> p h e", p=P))
        gate_rows = keep.tile([P, 2, T], F32, name="gate_rows")
        nc.sync.dma_start(out=gate_rows[:], in_=gate[:, 0:P, :].rearrange("r p t -> p r t"))
        ident = keep.tile([P, P], F32, name="ident")
        make_identity(nc, ident[:])
        pos_sb = []
        for r, pos in enumerate((pos1, pos2)):
            positions = keep.tile([P, T // PER_COLUMN], U16, name=f"pos_sb{r}")
            nc.sync.dma_start(positions[:], pos)
            pos_sb.append(positions)

        def quantise(values, width, name, tag=None):
            codes = keep.tile([P, width], U32, name=f"{name}_codes", tag=tag or f"{name}_codes", align_bytes=64)
            scales = keep.tile([P, width], U8, name=f"{name}_scales", align_bytes=64)
            nc.vector.quantize_mx(out=codes[:].bitcast(FP8X4), scales=scales[:], in_=values)
            return codes, scales

        wu_q = []
        for a in range(PASSES):
            grouped = keep.tile([P, K * PACK], BF16, name=f"wu_grouped{a}", align_bytes=64)
            dst = grouped[:].rearrange("p (t m j) -> p m j t", t=PACK, j=PACK)
            src = wu_raw[a][:].rearrange("p j (m t) -> p m j t", t=PACK)
            nc.vector.tensor_copy(out=dst[:, :, :, :2], in_=src[:, :, :, :2])
            nc.scalar.copy(out=dst[:, :, :, 2:], in_=src[:, :, :, 2:])
            wu_q.append(quantise(grouped[:], K, f"wu{a}"))

        pairs = [keep.tile([P, T * 2], BF16, name=f"pairs{g}", align_bytes=64) for g in range(2)]
        u_q = {}

        def prepare(a, t0, width):
            grouped = keep.tile([P, width * PACK], BF16, name=f"u_grouped{a}_{t0}", align_bytes=64)
            dst = grouped[:].rearrange("p (c i j) -> p c j i", i=4, j=PACK)
            src = u_raw[a, t0][:].rearrange("p j (c i) -> p c j i", i=4)
            cut = U_VECTOR // 4
            nc.vector.tensor_copy(out=dst[:, :cut], in_=src[:, :cut])
            if width > U_VECTOR:
                nc.scalar.copy(out=dst[:, cut:], in_=src[:, cut:])
            u_q[a, t0] = quantise(grouped[:], width, f"u{a}_{t0}")

        def project(bank, g, j, a, operand):
            codes, scales = operand
            cols = slice((2 * g + j) * P, (2 * g + j + 1) * P)
            nc.tensor.matmul_mx(
                out=bank[:, j, :],
                lhsT=wu_q[a][0][:, cols].bitcast(FP8X4),
                lhsT_scale=wu_q[a][1][:, cols],
                rhs=codes.bitcast(FP8X4),
                rhs_scale=scales,
                start=(a == 0),
                stop=(a == PASSES - 1),
            )

        def project_tokens(groups):
            x_banks = {}
            for g in range(2):
                for t0, width, operands in groups:
                    x_banks[g, t0] = psum.tile([P, 2, width], F32, name=f"x_bank{g}_{t0}")
                    project(x_banks[g, t0], g, 0, 0, operands[0])
            for g in range(2):
                for t0, width, operands in groups:
                    for j, a in ((0, 1), (1, 0), (1, 1)):
                        project(x_banks[g, t0], g, j, a, operands[a])
                    dst = pairs[g][:, 2 * t0:2 * (t0 + width)].rearrange("p (n j) -> p n j", j=2)
                    src = x_banks[g, t0][:].rearrange("p j n -> p n j")
                    if t0 == HALF:
                        nc.vector.tensor_copy(out=dst, in_=src)
                    else:
                        nc.scalar.copy(out=dst, in_=src)

        for piece in U_PIECES[:PASSES]:
            prepare(*piece)
        project_tokens([(0, HALF, [(u_q[a, 0][0][:], u_q[a, 0][1][:]) for a in range(PASSES)])])
        for piece in U_PIECES[PASSES:]:
            prepare(*piece)
        quarters = []
        for i in range(2):
            cols = slice(i * P, (i + 1) * P)
            early, final = u_q[0, HALF], u_q[1, HALF + i * P]
            quarters.append((HALF + i * P, P, [(early[0][:, cols], early[1][:, cols]), (final[0][:], final[1][:])]))
        project_tokens(quarters)

        y = [keep.tile([P, S], F32, name=f"y{nb}") for nb in range(2)]
        slot_q = []

        def expert(bank_cols, e, nb):
            codes, scales, first = slot_q[e]
            w0 = e * N + nb * P
            nc.tensor.matmul_mx(
                out=bank_cols,
                lhsT=ww[:, 2 * w0:2 * (w0 + P)].bitcast(FP4X4),
                lhsT_scale=ws[:, w0:w0 + P],
                rhs=codes[:, first:first + C].bitcast(FP8X4),
                rhs_scale=scales[:, first:first + C],
                start=True,
                stop=True,
            )

        def rectify(dst, bank_cols, e, nb):
            nc.scalar.activation(out=dst, in_=bank_cols, func=ACT.Relu, bias=bias[:, nb, e:e + 1])

        starts = [sum(CHUNKS[:c]) for c in range(len(CHUNKS))]
        last = len(CHUNKS) - 1
        picked = {}
        woven = {}

        def entries(c):
            return offs_sb[:, starts[c] // PER_COLUMN:(starts[c] + CHUNKS[c]) // PER_COLUMN]

        def new_woven(c):
            woven[c] = keep.tile([P, CHUNKS[c] * 2], U32, name=f"woven{c}", tag=WOVEN_TAGS[c], align_bytes=64)
            return woven[c][:].rearrange("p (n g) -> p n g", g=2)

        def gather(c):
            if c == last:
                side_by_side = new_woven(c)
                for g in range(2):
                    nc.vector.tensor_copy(out=side_by_side[:, :, g], in_=pairs[g][:].bitcast(U32).indirect(entries(c)))
                return
            picked[c] = keep.tile([P, 2, CHUNKS[c]], U32, name=f"picked{c}", tag=PICKED_TAGS[c], align_bytes=64)
            for g in range(2):
                nc.vector.tensor_copy(out=picked[c][:, g, :], in_=pairs[g][:].bitcast(U32).indirect(entries(c)))

        def weave(c):
            nc.scalar.copy(out=new_woven(c), in_=picked[c][:].rearrange("p g n -> p n g"))

        def multiply(c):
            width = CHUNKS[c]
            codes, scales = quantise(woven[c][:].bitcast(BF16), width, f"x{c}", "chain3" if c == last else None)
            bank = psum.tile([P, width], F32, name=f"y0_bank{c}", tag=Y0_BANKS[c])
            for i in range(width // C):
                slot_q.append((codes, scales, i * C))
                expert(bank[:, i * C:(i + 1) * C], starts[c] // C + i, 0)
            return bank

        def finish(c, bank):
            relu = keep.tile([P, CHUNKS[c]], F32, name=f"relu0{c}", tag=RELU_TAGS[c], align_bytes=64)
            for i in range(CHUNKS[c] // C):
                rectify(relu[:, i * C:(i + 1) * C], bank[:, i * C:(i + 1) * C], starts[c] // C + i, 0)
            nc.scalar.activation(out=y[0][:, starts[c]:starts[c] + CHUNKS[c]], in_=relu[:], func=ACT.Square)

        for c in range(2):
            gather(c)
            weave(c)
        for c in range(last - 1):
            chunk_bank = multiply(c)
            gather(c + 2)
            if c + 2 < last:
                weave(c + 2)
            finish(c, chunk_bank)
        last_banks = [multiply(c) for c in (last - 1, last)]
        relu_last = keep.tile([P, 2 * C], F32, name="relu_last", tag="chain2", align_bytes=64)
        for i in range(2):
            e = E - 2 + i
            cols = slice(i * C, (i + 1) * C)
            nc.vector.tensor_scalar(relu_last[:, cols], last_banks[i][:], bias[:, 0, e:e + 1], 0.0, ALU.add, ALU.max)
            nc.vector.tensor_tensor(y[0][:, e * C:(e + 1) * C], relu_last[:, cols], relu_last[:, cols], ALU.mult)

        relu1 = keep.tile([P, S], F32, name="relu1", tag="relu02", align_bytes=64)
        for q, tag in enumerate(Y1_BANKS):
            y1_bank = psum.tile([P, BANK_EXPERTS * C], F32, name=f"y1_bank{q}", tag=tag)
            for i in range(BANK_EXPERTS):
                expert(y1_bank[:, i * C:(i + 1) * C], BANK_EXPERTS * q + i, 1)
            for i in range(BANK_EXPERTS):
                e = BANK_EXPERTS * q + i
                rectify(relu1[:, e * C:(e + 1) * C], y1_bank[:, i * C:(i + 1) * C], e, 1)
            cols = slice(q * BANK_EXPERTS * C, (q + 1) * BANK_EXPERTS * C)
            nc.scalar.activation(out=y[1][:, cols], in_=relu1[:, cols], func=ACT.Square)

        terms = [keep.tile([P, 2, T], F32, name=f"terms{nb}") for nb in range(2)]

        def gated(nb, r):
            nc.vector.tensor_tensor(terms[nb][:, r, :], y[nb][:].indirect(pos_sb[r][:]), gate_rows[:, r, :], ALU.mult)

        sum_banks = [psum.tile([P, P], F32, name=f"turned_sum{i}", tag=SUM_BANKS[i]) for i in range(BLOCKS)]
        for r in range(2):
            gated(0, r)
            for i in range(BLOCKS):
                nc.tensor.matmul(
                    sum_banks[i][:], terms[0][:, r, i * P:(i + 1) * P], ident[:],
                    start=(r == 0), stop=(r == 1), is_transpose=True,
                )
        turned = keep.tile([P, T], F32, name="turned", tag="relu02", align_bytes=64)
        for i in range(BLOCKS):
            nc.scalar.copy(out=turned[:, i * P:(i + 1) * P], in_=sum_banks[i][:])
        total0 = keep.tile([P, T], F32, name="total0")
        for h, tag in enumerate(BACK_BANKS):
            back_bank = psum.tile([P, HALF], F32, name=f"sum0{h}", tag=tag)
            for i in range(2):
                cols = slice(h * HALF + i * P, h * HALF + (i + 1) * P)
                nc.tensor.transpose(back_bank[:, i * P:(i + 1) * P], turned[:, cols], ident[:])
            nc.scalar.copy(out=total0[:, h * HALF:(h + 1) * HALF], in_=back_bank[:])
        nc.sync.dma_start(out=out[0:P, :], in_=total0[:])

        for r in range(2):
            gated(1, r)
        total1 = keep.tile([P, T], F32, name="total1")
        for h in range(2):
            cols = slice(h * HALF, (h + 1) * HALF)
            nc.vector.tensor_tensor(total1[:, cols], terms[1][:, 0, cols], terms[1][:, 1, cols], ALU.add)
            nc.sync.dma_start(out=out[P:2 * P, cols], in_=total1[:, cols])
